import numpy as np
import ml_dtypes


def mxq(x, axis, fmt="e4m3"):
    dtype, down = {"e4m3": (ml_dtypes.float8_e4m3fn, 7), "e5m2": (ml_dtypes.float8_e5m2, 14)}[fmt]
    v = np.moveaxis(np.asarray(x, np.float32).astype(ml_dtypes.bfloat16).astype(np.float64), axis, -1)
    blocks = v.reshape(v.shape[:-1] + (-1, 32))
    amax = np.abs(blocks).max(-1, keepdims=True)
    byte = np.maximum(np.where(amax > 0, np.frexp(amax)[1] - 1 + 127, 0) - down, 1)
    scale = np.exp2(byte - 127.0)
    codes = (blocks / scale).astype(np.float32).astype(dtype).astype(np.float64)
    return np.moveaxis((codes * scale).reshape(v.shape), -1, axis)


WIDE = False


def mx_kscale(k):
    if not WIDE:
        return np.ones(k)
    levels = np.array([10, -10, 5, -5, 0])
    if k % 512:
        return np.exp2(np.random.permutation(np.resize(levels, k // 32))).repeat(32)
    a = np.empty((k // 512, 16))
    for p in range(k // 512):
        a[p, :8] = np.random.permutation(np.resize(levels, 8))
        for g in range(8):
            far = levels[np.abs(levels - a[p, g]) >= 10]
            a[p, g + 8] = far[np.random.randint(len(far))]
    return np.exp2(a.ravel()).repeat(32)


def f64(x):
    return np.asarray(x).astype(np.float64)


def striped(idx):
    return np.tile(idx.reshape(-1, 16).T, (8, 1)).astype(np.uint16)


def unstriped(offs):
    return offs[:16].T.reshape(-1).astype(np.int64)


E2M1 = np.array([0.0, 0.5, 1.0, 1.5, 2.0, 3.0, 4.0, 6.0, -0.0, -0.5, -1.0, -1.5, -2.0, -3.0, -4.0, -6.0])


def pack_weight(w, fmt):
    k, n = w.shape
    w = f64(np.asarray(w, np.float32).astype(ml_dtypes.bfloat16)).reshape(k // 32, 32, n)
    amax = np.abs(w).max(1)
    if fmt == "e4m3":
        byte = np.frexp(amax)[1] - 1 + 127 - 7
    else:
        mant, ex = np.frexp(amax / 6.0)
        byte = np.where(mant > 0.5, ex, ex - 1) + 127
    byte = np.clip(np.where(amax > 0, byte, 1), 1, 254)
    scaled = (w * np.exp2(127.0 - byte)[:, None, :]).reshape(k, n).astype(np.float32)
    by_word = np.ascontiguousarray(scaled.reshape(k // 512, 128, 4, n).transpose(0, 1, 3, 2))
    if fmt == "e4m3":
        words = by_word.astype(ml_dtypes.float8_e4m3fn).view(np.uint8)
    else:
        c = by_word.astype(ml_dtypes.float4_e2m1fn).view(np.uint8) & 0xF
        words = (c[..., 0::2] | (c[..., 1::2] << 4)).reshape(k // 512, 128, 2 * n)
    return np.ascontiguousarray(words), np.ascontiguousarray(byte.astype(np.uint8).reshape(k // 512, 16, n))


def unpack_weight(words, scales, fmt):
    g, _, n = scales.shape
    words = np.ascontiguousarray(words).reshape(g, 128, n, -1)
    if fmt == "e4m3":
        vals = words.view(ml_dtypes.float8_e4m3fn).astype(np.float64)
    else:
        nib = np.empty((g, 128, n, 4), np.uint8)
        nib[..., 0::2] = words & 0xF
        nib[..., 1::2] = words >> 4
        vals = E2M1[nib]
    vals = vals * np.repeat(np.exp2(scales.astype(np.float64) - 127.0), 8, axis=1)[..., None]
    return vals.transpose(0, 1, 3, 2).reshape(g * 512, n)


def gelu(v):
    return 0.5 * v * (1.0 + np.tanh(np.sqrt(2.0 / np.pi) * (v + 0.044715 * v**3)))


K, H, N, T, S, P, P2 = 1024, 1024, 512, 2048, 1024, 512, 256


def setup_inputs():
    n = np.random.standard_normal
    s = mx_kscale(K)[:, None]
    u = mx_kscale(H)[:, None]
    tab_words, tab_scales = pack_weight(n((K, T)) * s, "e4m3")
    w2_words, w2_scales = pack_weight(0.7 * n((K, H)) / np.sqrt(K) / s, "e2m1")
    faces = np.random.permutation(S)
    mates = np.random.permutation(P)
    return {
        "tab_words": tab_words,
        "tab_scales": tab_scales,
        "offs": striped(np.random.permutation(T)[:S]),
        "pos1": striped(faces[:P]),
        "pos2": striped(faces[P:P + P]),
        "pos3": striped(mates[:P2]),
        "pos4": striped(mates[P2:P2 + P2]),
        "w1": (1.7 * n((K, H)) / np.sqrt(K) / s).astype(np.float32),
        "w2_words": w2_words,
        "w2_scales": w2_scales,
        "gain": (np.exp(0.3 * n(H)) * u[:, 0]).astype(np.float32),
        "wo": (0.9 * n((H, N)) / np.sqrt(H) / u).astype(np.float32),
        "bo": (0.5 * n(N)).astype(np.float32),
    }


def reference(tab_words, tab_scales, offs, pos1, pos2, pos3, pos4, w1, w2_words, w2_scales, gain, wo, bo):
    v = unpack_weight(tab_words, tab_scales, "e4m3")[:, unstriped(offs)]
    w2 = unpack_weight(w2_words, w2_scales, "e2m1")
    rind = mxq(f64(w1), 0, "e4m3").T @ v
    body = w2.T @ v
    h = f64(gain)[:, None] * (np.tanh(rind) + body)
    d = h[:, unstriped(pos1)] - h[:, unstriped(pos2)]
    y = np.tanh((mxq(f64(wo), 0, "e4m3").T @ mxq(d, 0, "e4m3")) + f64(bo)[:, None])
    return np.minimum(y[:, unstriped(pos3)], y[:, unstriped(pos4)])

@@ -1,0 +1,296 @@
+from contextlib import ExitStack
+
+import concourse.mybir as mybir
+from concourse.masks import make_identity
+
+K, H, N, T, S, PAIRS, MATES = 1024, 1024, 512, 2048, 1024, 512, 256
+FLOPS = 2 * (2 * K * H * S + H * N * PAIRS)
+
+F32 = mybir.dt.float32
+BF16 = mybir.dt.bfloat16
+I32 = mybir.dt.int32
+U32 = mybir.dt.uint32
+U16 = mybir.dt.uint16
+U8 = mybir.dt.uint8
+FP8X4 = mybir.dt.float8_e4m3fn_x4
+FP4X4 = mybir.dt.float4_e2m1fn_x4
+ACT = mybir.ActivationFunctionType
+ALU = mybir.AluOpType
+
+P = 128
+PACK = 4
+PASS = P * PACK
+BANK = 512
+RUN = 8
+
+
+def tile_list_cheese_wheel_faces_kernel(
+    tc, tab_words, tab_scales, offs, pos1, pos2, pos3, pos4, w1, w2_words, w2_scales, gain, wo, bo, out
+):
+    nc = tc.nc
+    with ExitStack() as ctx:
+        keep = ctx.enter_context(tc.tile_pool(name="keep", bufs=1))
+        work = ctx.enter_context(tc.tile_pool(name="work", bufs=2))
+        psum = ctx.enter_context(tc.psum_pool(name="psum", bufs=1))
+
+        lists = {}
+        for name, src in (("offs", offs), ("pos1", pos1), ("pos2", pos2), ("pos3", pos3), ("pos4", pos4)):
+            lists[name] = keep.tile(list(src.shape), U16, name="list_" + name)
+
+        def load_list(name, src):
+            nc.sync.dma_start(lists[name][:], src)
+
+        tab_s = keep.tile([P, T], U8, name="tab_s", align_bytes=64)
+        tab_w = [keep.tile([P, T], I32, name="tab_w%d" % a, align_bytes=64) for a in range(2)]
+        picked_s = keep.tile([P, S], U8, name="picked_s", align_bytes=64)
+        v_s = keep.tile([P, 2 * S], U8, name="v_s", align_bytes=64)
+        v_w = [[keep.tile([P, BANK], U32, name="v_w%d%d" % (a, c), align_bytes=64) for c in range(2)] for a in range(2)]
+        w1_raw = [[keep.tile([P, PACK, PASS], F32, name="w1_raw%d%d" % (b, a)) for a in range(2)] for b in range(2)]
+        w2_raw = [keep.tile([P, 2, 256], I32, name="w2_raw%d" % b) for b in range(2)]
+        w2s_raw = keep.tile([P, 2, 256], I32, name="w2s_raw")
+        w2_w = [keep.tile([P, 2, 256], I32, name="w2_w%d" % b, align_bytes=64) for b in range(2)]
+        w2_s = keep.tile([P, 2, 256], I32, name="w2_s", align_bytes=64)
+        wo_all = [keep.tile([P, PACK, N], F32, name="wo_all%d" % b) for b in range(2)]
+        vec_rows = keep.tile([P, P], F32, name="vec_rows")
+        ident = keep.tile([P, P], F32, name="ident")
+        vec = keep.tile([P, 12], F32, name="vec")
+
+        nc.vector.memset(tab_s[0:96, :].bitcast(I32), 0)
+        nc.gpsimd.memset(w2s_raw[:], 0)
+        nc.gpsimd.memset(vec_rows[:], 0.0)
+        make_identity(nc, ident[:])
+        nc.gpsimd.memset(v_s[:].bitcast(I32), 0)
+        for q in range(4):
+            nc.scalar.dma_start(
+                w2s_raw[32 * q : 32 * q + 4, :, :],
+                w2_scales[:, 4 * q : 4 * q + 4, :].bitcast(I32).rearrange("a r c -> r a c"),
+            )
+        for b in range(2):
+            nc.gpsimd.dma_start(
+                vec_rows[4 * b : 4 * b + 4, :],
+                gain[PASS * b : PASS * (b + 1)].rearrange("(g t i) -> t g i", t=PACK, i=RUN),
+            )
+        nc.gpsimd.dma_start(vec_rows[8:12, :], bo.rearrange("(j p) -> j p", p=P))
+
+        def load_w1(b, a):
+            nc.sync.dma_start(
+                w1_raw[b][a][:],
+                w1[PASS * a : PASS * (a + 1), PASS * b : PASS * (b + 1)].rearrange("(p j) c -> p j c", j=PACK),
+            )
+
+        def load_w2(b):
+            nc.sync.dma_start(
+                w2_raw[b][:], w2_words[:, :, 1024 * b : 1024 * (b + 1)].bitcast(I32).rearrange("a p c -> p a c")
+            )
+
+        def load_tab(a):
+            nc.sync.dma_start(tab_w[a][:], tab_words[a].rearrange("p t i -> p (t i)").bitcast(I32))
+
+        def load_wo(b):
+            rows = wo[PASS * b : PASS * (b + 1), :].rearrange("(g t i) n -> t g i n", t=PACK, i=RUN)
+            for t in range(PACK):
+                nc.sync.dma_start(wo_all[b][:, t, :], rows[t])
+
+        load_list("offs", offs)
+        nc.sync.dma_start(tab_s[96:128, :].bitcast(I32), tab_scales.bitcast(I32).rearrange("a q c -> q a c"))
+        load_tab(0)
+        load_w1(0, 0)
+        load_w1(0, 1)
+        load_tab(1)
+        load_w2(0)
+        load_list("pos1", pos1)
+        load_list("pos2", pos2)
+        load_w2(1)
+        load_w1(1, 0)
+        load_w1(1, 1)
+        load_wo(0)
+        load_wo(1)
+        load_list("pos3", pos3)
+        load_list("pos4", pos4)
+
+        nc.vector.tensor_copy(picked_s[:], tab_s[:].indirect(lists["offs"][:]))
+        for q in range(4):
+            nc.scalar.dma_start(
+                v_s[32 * q : 32 * q + 4, :].bitcast(I32), picked_s[96 + 8 * q : 96 + 8 * q + 8, :].bitcast(I32)
+            )
+
+        def gather_words(a, c):
+            nc.vector.tensor_copy(
+                v_w[a][c][:], tab_w[a][:].bitcast(U32).indirect(lists["offs"][:, 32 * c : 32 * (c + 1)])
+            )
+
+        def deal_w2_words(b):
+            nc.vector.tensor_copy(
+                w2_w[b][:].rearrange("p a (t g w) -> p a t g w", t=PACK, w=4),
+                w2_raw[b][:].rearrange("p a (g t w) -> p a t g w", t=PACK, w=4),
+            )
+
+        def deal_w2_scales():
+            nc.vector.tensor_copy(
+                w2_s[:].rearrange("p a (b t g w) -> p (a b) t g w", b=2, t=PACK, w=2),
+                w2s_raw[:].rearrange("p a (b g t w) -> p (a b) t g w", b=2, t=PACK, w=2),
+            )
+
+        w1_w = {}
+        w1_s = {}
+        w1_bf = {}
+
+        def cast_w1(b, t, a):
+            if a == 0:
+                w1_bf[b, t] = work.tile([P, 2, PASS], BF16, name="w1_bf", bufs=4, align_bytes=64)
+            nc.scalar.copy(
+                w1_bf[b, t][:, a, :].rearrange("p (g u i j) -> p g u j i", u=2, i=4, j=PACK),
+                w1_raw[b][a][:].rearrange("p j (g t u i) -> p t g u j i", t=PACK, u=2, i=4)[:, t],
+            )
+
+        def quantise_w1(b, t):
+            w1_w[b, t] = keep.tile([P, 2 * P], U32, name="w1_w%d%d" % (b, t), align_bytes=64)
+            w1_s[b, t] = keep.tile([P, 2 * P], U8, name="w1_s%d%d" % (b, t), align_bytes=64)
+            nc.vector.quantize_mx(
+                out=w1_w[b, t][:].bitcast(FP8X4),
+                scales=w1_s[b, t][:],
+                in_=w1_bf[b, t][:].rearrange("p a c -> p (a c)"),
+            )
+
+        wo_w = [keep.tile([P, N], U32, name="wo_w%d" % b, align_bytes=64) for b in range(2)]
+        wo_s = [keep.tile([P, N], U8, name="wo_s%d" % b, align_bytes=64) for b in range(2)]
+        wo_bf = [keep.tile([P, PACK * N], BF16, name="wo_bf%d" % b, align_bytes=64) for b in range(2)]
+
+        def cast_wo(b, part):
+            cols = slice(part * 64, (part + 1) * 64)
+            nc.scalar.copy(
+                wo_bf[b][:].rearrange("p (c i t) -> p c t i", i=4, t=PACK)[:, cols],
+                wo_all[b][:].rearrange("p t (c i) -> p c t i", i=4)[:, cols],
+            )
+
+        def quantise_wo(b):
+            nc.vector.quantize_mx(out=wo_w[b][:].bitcast(FP8X4), scales=wo_s[b][:], in_=wo_bf[b][:])
+
+        h = {}
+        bank_count = [0]
+
+        def bank():
+            bank_count[0] = bank_count[0] + 1
+            return psum.tile([P, BANK], F32, name="bank", tag="bank%d" % (bank_count[0] % 8))
+
+        def stage1(b, t, c):
+            if c == 0:
+                h[b, t] = work.tile([P, S], F32, name="h", bufs=3)
+            rind = bank()
+            body = bank()
+            for a in range(2):
+                nc.tensor.matmul_mx(
+                    out=rind[:],
+                    lhsT=w1_w[b, t][:, P * a : P * (a + 1)].bitcast(FP8X4),
+                    lhsT_scale=w1_s[b, t][:, P * a : P * (a + 1)],
+                    rhs=v_w[a][c][:].bitcast(FP8X4),
+                    rhs_scale=v_s[:, S * a + BANK * c : S * a + BANK * (c + 1)],
+                    start=(a == 0),
+                    stop=(a == 1),
+                )
+            for a in range(2):
+                nc.tensor.matmul_mx(
+                    out=body[:],
+                    lhsT=w2_w[b][:, a, 64 * t : 64 * (t + 1)].bitcast(U8).bitcast(FP4X4),
+                    lhsT_scale=w2_s[:, a, 128 * b + 32 * t : 128 * b + 32 * (t + 1)].bitcast(U8),
+                    rhs=v_w[a][c][:].bitcast(FP8X4),
+                    rhs_scale=v_s[:, S * a + BANK * c : S * a + BANK * (c + 1)],
+                    start=(a == 0),
+                    stop=(a == 1),
+                )
+            th = work.tile([P, BANK], F32, name="th", bufs=4)
+            nc.scalar.activation(th[:], rind[:], ACT.Tanh)
+            nc.vector.tensor_tensor(h[b, t][:, BANK * c : BANK * (c + 1)], body[:], th[:], ALU.add)
+
+        d_bf = [keep.tile([P, PACK, PAIRS], BF16, name="d_bf%d" % b) for b in range(2)]
+        d_w = [keep.tile([P, PAIRS], U32, name="d_w%d" % b, align_bytes=64) for b in range(2)]
+        d_s = [keep.tile([P, PAIRS], U8, name="d_s%d" % b, align_bytes=64) for b in range(2)]
+
+        def difference(b, t, m0, m1):
+            width = m1 - m0
+            second = work.tile([P, width], F32, name="second", bufs=3)
+            diff = work.tile([P, width], F32, name="diff", bufs=3)
+            nc.vector.tensor_copy(second[:], h[b, t][:].indirect(lists["pos2"][:, m0 // 16 : m1 // 16]))
+            nc.vector.tensor_tensor(
+                diff[:], h[b, t][:].indirect(lists["pos1"][:, m0 // 16 : m1 // 16]), second[:], ALU.subtract
+            )
+            nc.scalar.activation(d_bf[b][:, t, m0:m1], diff[:], ACT.Copy, scale=vec[:, 4 * b + t : 4 * b + t + 1])
+
+        def quantise_d(b, m0, m1):
+            width = m1 - m0
+            woven = work.tile([P, PACK * width], BF16, name="woven", bufs=2, align_bytes=64)
+            nc.scalar.copy(
+                woven[:].rearrange("p (c i t) -> p c t i", i=4, t=PACK),
+                d_bf[b][:, :, m0:m1].rearrange("p t (c i) -> p c t i", i=4),
+            )
+            nc.vector.quantize_mx(out=d_w[b][:, m0:m1].bitcast(FP8X4), scales=d_s[b][:, m0:m1], in_=woven[:])
+
+        y = [keep.tile([P, PAIRS], F32, name="y%d" % j) for j in range(4)]
+
+        def stage2(j, m0, m1):
+            acc = bank()
+            for b in range(2):
+                nc.tensor.matmul_mx(
+                    out=acc[:, 0 : m1 - m0],
+                    lhsT=wo_w[b][:, P * j : P * (j + 1)].bitcast(FP8X4),
+                    lhsT_scale=wo_s[b][:, P * j : P * (j + 1)],
+                    rhs=d_w[b][:, m0:m1].bitcast(FP8X4),
+                    rhs_scale=d_s[b][:, m0:m1],
+                    start=(b == 0),
+                    stop=(b == 1),
+                )
+            nc.scalar.activation(y[j][:, m0:m1], acc[:, 0 : m1 - m0], ACT.Tanh, bias=vec[:, 8 + j : 9 + j])
+
+        def mates(j):
+            left = work.tile([P, MATES], F32, name="left")
+            right = work.tile([P, MATES], F32, name="right")
+            least = work.tile([P, MATES], F32, name="least", bufs=4)
+            nc.vector.tensor_copy(left[:], y[j][:].indirect(lists["pos3"][:]))
+            nc.vector.tensor_copy(right[:], y[j][:].indirect(lists["pos4"][:]))
+            nc.vector.tensor_tensor(least[:], left[:], right[:], ALU.min)
+            nc.sync.dma_start(out[P * j : P * (j + 1), :], least[:])
+
+        turned = bank()
+        nc.tensor.transpose(turned[:, 0:P], vec_rows[:], ident[:])
+        nc.scalar.copy(vec[:], turned[:, 0:12])
+        gather_words(0, 0)
+        gather_words(0, 1)
+        deal_w2_scales()
+        for t in range(PACK):
+            cast_w1(0, t, 0)
+        for t in range(PACK):
+            cast_w1(0, t, 1)
+            quantise_w1(0, t)
+        gather_words(1, 0)
+        deal_w2_words(0)
+        gather_words(1, 1)
+
+        slices = [(b, t) for b in range(2) for t in range(PACK)]
+        for n, (b, t) in enumerate(slices):
+            stage1(b, t, 0)
+            stage1(b, t, 1)
+            if b == 0:
+                cast_w1(1, t, 0)
+                cast_w1(1, t, 1)
+                quantise_w1(1, t)
+            else:
+                cast_wo(t // 2, t % 2)
+                if t % 2 == 1:
+                    quantise_wo(t // 2)
+            if n == 0:
+                deal_w2_words(1)
+            if 1 <= n <= 6:
+                pb, pt = slices[n - 1]
+                difference(pb, pt, 0, PAIRS)
+            if n == 5:
+                quantise_d(0, 0, PAIRS)
+        half = PAIRS // 2
+        for m0 in (0, half):
+            difference(1, 2, m0, m0 + half)
+            difference(1, 3, m0, m0 + half)
+        for m0 in (0, half):
+            quantise_d(1, m0, m0 + half)
+            for j in range(4):
+                stage2(j, m0, m0 + half)
+        for j in range(4):
+            mates(j)

@@ -22,6 +22,9 @@ PACK = 4
 PASS = P * PACK
 BANK = 512
 RUN = 8
+WO_SHARE = (0, 0, 0, 1, 1, 1, 0, 5)
+PARTS = 2
+PIECES = ((0, 128), (128, 256), (256, 384), (384, 512))
 
 
 def tile_list_cheese_wheel_faces_kernel(
@@ -40,111 +43,112 @@ def tile_list_cheese_wheel_faces_kernel(
         def load_list(name, src):
             nc.sync.dma_start(lists[name][:], src)
 
-        tab_s = keep.tile([P, T], U8, name="tab_s", align_bytes=64)
+        tab_s = work.tile([P, T], U8, name="tab_s", tag="early", bufs=1, align_bytes=64)
         tab_w = [keep.tile([P, T], I32, name="tab_w%d" % a, align_bytes=64) for a in range(2)]
         picked_s = keep.tile([P, S], U8, name="picked_s", align_bytes=64)
-        v_s = keep.tile([P, 2 * S], U8, name="v_s", align_bytes=64)
+        stage = keep.tile([P, 512], I32, name="stage")
+        planes = keep.tile([P, 2, 512], I32, name="planes", align_bytes=64)
         v_w = [[keep.tile([P, BANK], U32, name="v_w%d%d" % (a, c), align_bytes=64) for c in range(2)] for a in range(2)]
-        w1_raw = [[keep.tile([P, PACK, PASS], F32, name="w1_raw%d%d" % (b, a)) for a in range(2)] for b in range(2)]
-        w2_raw = [keep.tile([P, 2, 256], I32, name="w2_raw%d" % b) for b in range(2)]
-        w2s_raw = keep.tile([P, 2, 256], I32, name="w2s_raw")
-        w2_w = [keep.tile([P, 2, 256], I32, name="w2_w%d" % b, align_bytes=64) for b in range(2)]
-        w2_s = keep.tile([P, 2, 256], I32, name="w2_s", align_bytes=64)
-        wo_all = [keep.tile([P, PACK, N], F32, name="wo_all%d" % b) for b in range(2)]
-        vec_rows = keep.tile([P, P], F32, name="vec_rows")
+        w1_raw = {}
+        w2_raw = keep.tile([P, 2, 512], I32, name="w2_raw", align_bytes=64)
+        w2_dealt = keep.tile([P, 2, 256], I32, name="w2_dealt", align_bytes=64)
+        w2s_dealt = keep.tile([P, 2, 128], I32, name="w2s_dealt", align_bytes=64)
+        wo_all = {}
         ident = keep.tile([P, P], F32, name="ident")
         vec = keep.tile([P, 12], F32, name="vec")
 
-        nc.vector.memset(tab_s[0:96, :].bitcast(I32), 0)
-        nc.gpsimd.memset(w2s_raw[:], 0)
-        nc.gpsimd.memset(vec_rows[:], 0.0)
+        warm = keep.tile([P, 16], F32, name="warm")
+        nc.gpsimd.memset(warm[:, 0:8], 0.0)
+        nc.scalar.activation(warm[:, 8:9], warm[:, 0:1], ACT.Tanh)
+        nc.gpsimd.memset(tab_s[0:96, :].bitcast(I32), 0)
+        nc.gpsimd.memset(planes[:], 0)
         make_identity(nc, ident[:])
-        nc.gpsimd.memset(v_s[:].bitcast(I32), 0)
-        for q in range(4):
-            nc.scalar.dma_start(
-                w2s_raw[32 * q : 32 * q + 4, :, :],
-                w2_scales[:, 4 * q : 4 * q + 4, :].bitcast(I32).rearrange("a r c -> r a c"),
-            )
-        for b in range(2):
-            nc.gpsimd.dma_start(
-                vec_rows[4 * b : 4 * b + 4, :],
-                gain[PASS * b : PASS * (b + 1)].rearrange("(g t i) -> t g i", t=PACK, i=RUN),
-            )
-        nc.gpsimd.dma_start(vec_rows[8:12, :], bo.rearrange("(j p) -> j p", p=P))
 
-        def load_w1(b, a):
-            nc.sync.dma_start(
-                w1_raw[b][a][:],
-                w1[PASS * a : PASS * (a + 1), PASS * b : PASS * (b + 1)].rearrange("(p j) c -> p j c", j=PACK),
-            )
-
-        def load_w2(b):
-            nc.sync.dma_start(
-                w2_raw[b][:], w2_words[:, :, 1024 * b : 1024 * (b + 1)].bitcast(I32).rearrange("a p c -> p a c")
-            )
+        def load_w1(first, count):
+            for a in range(2):
+                w1_raw[first, a] = keep.tile([P, PACK, count * P], F32, name="w1_raw%d%d" % (first, a))
+                nc.sync.dma_start(
+                    w1_raw[first, a][:],
+                    w1[PASS * a : PASS * (a + 1), P * first : P * (first + count)].rearrange("(p j) c -> p j c", j=PACK),
+                )
 
         def load_tab(a):
             nc.sync.dma_start(tab_w[a][:], tab_words[a].rearrange("p t i -> p (t i)").bitcast(I32))
 
-        def load_wo(b):
-            rows = wo[PASS * b : PASS * (b + 1), :].rearrange("(g t i) n -> t g i n", t=PACK, i=RUN)
+        def load_wo():
+            for b in range(2):
+                wo_all[b] = keep.tile([P, PACK, N], F32, name="wo_raw%d" % b)
+            nc.sync.dma_start(wo_all[0][:], wo[0:PASS, :].rearrange("(p t) n -> p t n", t=PACK))
+            rows = wo[PASS : 2 * PASS, :].rearrange("(g t i) n -> t g i n", t=PACK, i=RUN)
             for t in range(PACK):
-                nc.sync.dma_start(wo_all[b][:, t, :], rows[t])
+                nc.sync.dma_start(wo_all[1][:, t, :], rows[t])
 
         load_list("offs", offs)
         nc.sync.dma_start(tab_s[96:128, :].bitcast(I32), tab_scales.bitcast(I32).rearrange("a q c -> q a c"))
-        load_tab(0)
-        load_w1(0, 0)
-        load_w1(0, 1)
-        load_tab(1)
-        load_w2(0)
+        nc.sync.dma_start(stage[96:128, 256:512], w2_scales.bitcast(I32).rearrange("a q c -> q a c"))
         load_list("pos1", pos1)
         load_list("pos2", pos2)
-        load_w2(1)
-        load_w1(1, 0)
-        load_w1(1, 1)
-        load_wo(0)
-        load_wo(1)
         load_list("pos3", pos3)
         load_list("pos4", pos4)
+        load_tab(0)
+        load_w1(0, 1)
+        load_tab(1)
+        nc.sync.dma_start(w2_raw[:], w2_words.bitcast(I32).rearrange("a p c -> p a c"))
+        load_w1(1, 1)
 
         nc.vector.tensor_copy(picked_s[:], tab_s[:].indirect(lists["offs"][:]))
+        nc.vector.tensor_copy(stage[96:128, 0:256], picked_s[96:128, :].bitcast(I32))
         for q in range(4):
-            nc.scalar.dma_start(
-                v_s[32 * q : 32 * q + 4, :].bitcast(I32), picked_s[96 + 8 * q : 96 + 8 * q + 8, :].bitcast(I32)
-            )
+            (nc.gpsimd, nc.scalar)[q % 2].dma_start(planes[32 * q : 32 * q + 4, :, :], stage[96 + 8 * q : 96 + 8 * q + 8, :])
+
+        load_w1(2, 2)
+        load_w1(4, 4)
+        load_wo()
+
+        vec_rows = work.tile([P, P], F32, name="vec_rows", tag="early", bufs=1, align_bytes=64)
+        nc.gpsimd.memset(vec_rows[:], 0.0)
+        nc.gpsimd.dma_start(vec_rows[0:4, :], gain[0:PASS].rearrange("(t p) -> t p", p=P))
+        nc.gpsimd.dma_start(vec_rows[4:8, :], gain[PASS : 2 * PASS].rearrange("(g t i) -> t g i", t=PACK, i=RUN))
+        nc.gpsimd.dma_start(vec_rows[8:12, :], bo.rearrange("(j p) -> j p", p=P))
 
         def gather_words(a, c):
             nc.vector.tensor_copy(
                 v_w[a][c][:], tab_w[a][:].bitcast(U32).indirect(lists["offs"][:, 32 * c : 32 * (c + 1)])
             )
 
-        def deal_w2_words(b):
+        def deal_w2():
             nc.vector.tensor_copy(
-                w2_w[b][:].rearrange("p a (t g w) -> p a t g w", t=PACK, w=4),
-                w2_raw[b][:].rearrange("p a (g t w) -> p a t g w", t=PACK, w=4),
+                w2_dealt[:].rearrange("p a (t g w) -> p a t g w", t=PACK, w=4),
+                w2_raw[:, :, 256:512].rearrange("p a (g t w) -> p a t g w", t=PACK, w=4),
+            )
+            nc.vector.tensor_copy(
+                w2s_dealt[:].rearrange("p a (t g w) -> p a t g w", t=PACK, w=2),
+                planes[:, :, 384:512].rearrange("p a (g t w) -> p a t g w", t=PACK, w=2),
             )
 
-        def deal_w2_scales():
-            nc.vector.tensor_copy(
-                w2_s[:].rearrange("p a (b t g w) -> p (a b) t g w", b=2, t=PACK, w=2),
-                w2s_raw[:].rearrange("p a (b g t w) -> p (a b) t g w", b=2, t=PACK, w=2),
-            )
+        w2_w = [w2_raw[:, :, 0:256], w2_dealt[:]]
+        w2_s = [planes[:, :, 256:384], w2s_dealt[:]]
 
         w1_w = {}
         w1_s = {}
         w1_bf = {}
 
-        def cast_w1(b, t, a):
+        def cast_w1(b, t, a, copy=nc.scalar.copy):
             if a == 0:
-                w1_bf[b, t] = work.tile([P, 2, PASS], BF16, name="w1_bf", bufs=4, align_bytes=64)
-            nc.scalar.copy(
-                w1_bf[b, t][:, a, :].rearrange("p (g u i j) -> p g u j i", u=2, i=4, j=PACK),
-                w1_raw[b][a][:].rearrange("p j (g t u i) -> p t g u j i", t=PACK, u=2, i=4)[:, t],
-            )
+                w1_bf[b, t] = work.tile([P, 2, PASS], BF16, name="w1_bf", tag="ring", bufs=3, align_bytes=64)
+            if b == 0:
+                copy(
+                    w1_bf[b, t][:, a, :].rearrange("p (c i j) -> p c j i", i=4, j=PACK),
+                    w1_raw[min(t, 2), a][:, :, P * max(t - 2, 0) : P * max(t - 1, 1)].rearrange("p j (c i) -> p c j i", i=4),
+                )
+            else:
+                nc.scalar.copy(
+                    w1_bf[b, t][:, a, :].rearrange("p (g u i j) -> p g u j i", u=2, i=4, j=PACK),
+                    w1_raw[4, a][:].rearrange("p j (g t u i) -> p t g u j i", t=PACK, u=2, i=4)[:, t],
+                )
 
         def quantise_w1(b, t):
-            w1_w[b, t] = keep.tile([P, 2 * P], U32, name="w1_w%d%d" % (b, t), align_bytes=64)
+            w1_w[b, t] = work.tile([P, 2 * P], U32, name="w1_w", tag="ring", bufs=3, align_bytes=64)
             w1_s[b, t] = keep.tile([P, 2 * P], U8, name="w1_s%d%d" % (b, t), align_bytes=64)
             nc.vector.quantize_mx(
                 out=w1_w[b, t][:].bitcast(FP8X4),
@@ -157,7 +161,7 @@ def tile_list_cheese_wheel_faces_kernel(
         wo_bf = [keep.tile([P, PACK * N], BF16, name="wo_bf%d" % b, align_bytes=64) for b in range(2)]
 
         def cast_wo(b, part):
-            cols = slice(part * 64, (part + 1) * 64)
+            cols = slice(part * 32, (part + 1) * 32)
             nc.scalar.copy(
                 wo_bf[b][:].rearrange("p (c i t) -> p c t i", i=4, t=PACK)[:, cols],
                 wo_all[b][:].rearrange("p t (c i) -> p c t i", i=4)[:, cols],
@@ -173,72 +177,90 @@ def tile_list_cheese_wheel_faces_kernel(
             bank_count[0] = bank_count[0] + 1
             return psum.tile([P, BANK], F32, name="bank", tag="bank%d" % (bank_count[0] % 8))
 
-        def stage1(b, t, c):
-            if c == 0:
-                h[b, t] = work.tile([P, S], F32, name="h", bufs=3)
-            rind = bank()
-            body = bank()
-            for a in range(2):
+        def stage1(b, t, order):
+            h[b, t] = work.tile([P, S], F32, name="h", bufs=4)
+            banks = {(kind, c): bank() for c in range(2) for kind in range(2)}
+            for kind, c, a in order:
+                if kind == 0:
+                    words = w1_w[b, t][:, P * a : P * (a + 1)].bitcast(FP8X4)
+                    scales = w1_s[b, t][:, P * a : P * (a + 1)]
+                else:
+                    words = w2_w[b][:, a, 64 * t : 64 * (t + 1)].bitcast(U8).bitcast(FP4X4)
+                    scales = w2_s[b][:, a, 32 * t : 32 * (t + 1)].bitcast(U8)
                 nc.tensor.matmul_mx(
-                    out=rind[:],
-                    lhsT=w1_w[b, t][:, P * a : P * (a + 1)].bitcast(FP8X4),
-                    lhsT_scale=w1_s[b, t][:, P * a : P * (a + 1)],
+                    out=banks[kind, c][:],
+                    lhsT=words,
+                    lhsT_scale=scales,
                     rhs=v_w[a][c][:].bitcast(FP8X4),
-                    rhs_scale=v_s[:, S * a + BANK * c : S * a + BANK * (c + 1)],
+                    rhs_scale=planes[:, a, P * c : P * (c + 1)].bitcast(U8),
                     start=(a == 0),
                     stop=(a == 1),
                 )
-            for a in range(2):
-                nc.tensor.matmul_mx(
-                    out=body[:],
-                    lhsT=w2_w[b][:, a, 64 * t : 64 * (t + 1)].bitcast(U8).bitcast(FP4X4),
-                    lhsT_scale=w2_s[:, a, 128 * b + 32 * t : 128 * b + 32 * (t + 1)].bitcast(U8),
-                    rhs=v_w[a][c][:].bitcast(FP8X4),
-                    rhs_scale=v_s[:, S * a + BANK * c : S * a + BANK * (c + 1)],
-                    start=(a == 0),
-                    stop=(a == 1),
-                )
-            th = work.tile([P, BANK], F32, name="th", bufs=4)
-            nc.scalar.activation(th[:], rind[:], ACT.Tanh)
-            nc.vector.tensor_tensor(h[b, t][:, BANK * c : BANK * (c + 1)], body[:], th[:], ALU.add)
+            for c in range(2):
+                th = work.tile([P, BANK], F32, name="th", bufs=4)
+                nc.scalar.activation(th[:], banks[0, c][:], ACT.Tanh)
+                nc.vector.tensor_tensor(h[b, t][:, BANK * c : BANK * (c + 1)], banks[1, c][:], th[:], ALU.add)
 
-        d_bf = [keep.tile([P, PACK, PAIRS], BF16, name="d_bf%d" % b) for b in range(2)]
+        d_rows = [keep.tile([P, PACK, PAIRS], BF16, name="d_rows%d" % b) for b in range(2)]
+        woven = [keep.tile([P, PAIRS, PACK], BF16, name="woven%d" % b, align_bytes=64) for b in range(2)]
         d_w = [keep.tile([P, PAIRS], U32, name="d_w%d" % b, align_bytes=64) for b in range(2)]
         d_s = [keep.tile([P, PAIRS], U8, name="d_s%d" % b, align_bytes=64) for b in range(2)]
 
-        def difference(b, t, m0, m1):
+        def difference(b, t, m0, m1, parts, second=None):
             width = m1 - m0
-            second = work.tile([P, width], F32, name="second", bufs=3)
-            diff = work.tile([P, width], F32, name="diff", bufs=3)
-            nc.vector.tensor_copy(second[:], h[b, t][:].indirect(lists["pos2"][:, m0 // 16 : m1 // 16]))
-            nc.vector.tensor_tensor(
-                diff[:], h[b, t][:].indirect(lists["pos1"][:, m0 // 16 : m1 // 16]), second[:], ALU.subtract
+            step = width // parts
+            if second is None:
+                second = work.tile([P, width], F32, name="second", bufs=4)
+            diff = work.tile([P, width], F32, name="diff", bufs=6)
+            for u in range(parts):
+                cols = slice((m0 + u * step) // 16, (m0 + (u + 1) * step) // 16)
+                nc.vector.tensor_copy(second[:, u * step : (u + 1) * step], h[b, t][:].indirect(lists["pos2"][:, cols]))
+            for u in range(parts):
+                cols = slice((m0 + u * step) // 16, (m0 + (u + 1) * step) // 16)
+                nc.vector.tensor_tensor(
+                    diff[:, u * step : (u + 1) * step],
+                    h[b, t][:].indirect(lists["pos1"][:, cols]),
+                    second[:, u * step : (u + 1) * step],
+                    ALU.subtract,
+                )
+            return diff
+
+        def scale(b, t, m0, m1, diff):
+            factor = vec[:, 4 * b + t : 4 * b + t + 1]
+            if b == 0:
+                rows = work.tile([P, PAIRS], BF16, name="rows", bufs=4)
+                nc.scalar.activation(rows[:], diff[:], ACT.Copy, scale=factor)
+                nc.sync.dma_start(d_rows[0][32 * t : 32 * (t + 1), :, :], rows[:])
+            else:
+                nc.scalar.activation(d_rows[1][:, t, m0:m1], diff[:], ACT.Copy, scale=factor)
+
+        def weave(b, m0, m1):
+            nc.scalar.copy(
+                woven[b][:, m0:m1, :].rearrange("p (c i) t -> p c t i", i=4),
+                d_rows[b][:, :, m0:m1].rearrange("p t (c i) -> p c t i", i=4),
             )
-            nc.scalar.activation(d_bf[b][:, t, m0:m1], diff[:], ACT.Copy, scale=vec[:, 4 * b + t : 4 * b + t + 1])
 
         def quantise_d(b, m0, m1):
-            width = m1 - m0
-            woven = work.tile([P, PACK * width], BF16, name="woven", bufs=2, align_bytes=64)
-            nc.scalar.copy(
-                woven[:].rearrange("p (c i t) -> p c t i", i=4, t=PACK),
-                d_bf[b][:, :, m0:m1].rearrange("p t (c i) -> p c t i", i=4),
+            nc.vector.quantize_mx(
+                out=d_w[b][:, m0:m1].bitcast(FP8X4),
+                scales=d_s[b][:, m0:m1],
+                in_=woven[b][:, m0:m1, :].rearrange("p m t -> p (m t)"),
             )
-            nc.vector.quantize_mx(out=d_w[b][:, m0:m1].bitcast(FP8X4), scales=d_s[b][:, m0:m1], in_=woven[:])
 
         y = [keep.tile([P, PAIRS], F32, name="y%d" % j) for j in range(4)]
 
-        def stage2(j, m0, m1):
-            acc = bank()
-            for b in range(2):
-                nc.tensor.matmul_mx(
-                    out=acc[:, 0 : m1 - m0],
-                    lhsT=wo_w[b][:, P * j : P * (j + 1)].bitcast(FP8X4),
-                    lhsT_scale=wo_s[b][:, P * j : P * (j + 1)],
-                    rhs=d_w[b][:, m0:m1].bitcast(FP8X4),
-                    rhs_scale=d_s[b][:, m0:m1],
-                    start=(b == 0),
-                    stop=(b == 1),
-                )
+        def stage2(acc, j, b, m0, m1, first, start, stop):
+            nc.tensor.matmul_mx(
+                out=acc[:, m0 - first : m1 - first],
+                lhsT=wo_w[b][:, P * j : P * (j + 1)].bitcast(FP8X4),
+                lhsT_scale=wo_s[b][:, P * j : P * (j + 1)],
+                rhs=d_w[b][:, m0:m1].bitcast(FP8X4),
+                rhs_scale=d_s[b][:, m0:m1],
+                start=start,
+                stop=stop,
+            )
+
+        def finish(acc, j, m0, m1):
             nc.scalar.activation(y[j][:, m0:m1], acc[:, 0 : m1 - m0], ACT.Tanh, bias=vec[:, 8 + j : 9 + j])
 
         def mates(j):
@@ -250,47 +272,82 @@ def tile_list_cheese_wheel_faces_kernel(
             nc.vector.tensor_tensor(least[:], left[:], right[:], ALU.min)
             nc.sync.dma_start(out[P * j : P * (j + 1), :], least[:])
 
-        turned = bank()
-        nc.tensor.transpose(turned[:, 0:P], vec_rows[:], ident[:])
-        nc.scalar.copy(vec[:], turned[:, 0:12])
+        def turn_vectors():
+            turned = bank()
+            nc.tensor.transpose(turned[:, 0:P], vec_rows[:], ident[:])
+            nc.scalar.copy(vec[:], turned[:, 0:12])
+
         gather_words(0, 0)
         gather_words(0, 1)
-        deal_w2_scales()
-        for t in range(PACK):
-            cast_w1(0, t, 0)
-        for t in range(PACK):
-            cast_w1(0, t, 1)
-            quantise_w1(0, t)
+        cast_w1(0, 0, 0)
+        cast_w1(0, 0, 1)
+        quantise_w1(0, 0)
         gather_words(1, 0)
-        deal_w2_words(0)
         gather_words(1, 1)
+        deal_w2()
 
         slices = [(b, t) for b in range(2) for t in range(PACK)]
+        by_half = [(kind, c, a) for c in range(2) for kind in range(2) for a in range(2)]
+        first_pass_first = [x for x in by_half if x[2] == 0] + [x for x in by_half if x[2] == 1]
+        wo_parts = [(b, part) for b in range(2) for part in range(4)]
+        diffs = {}
         for n, (b, t) in enumerate(slices):
-            stage1(b, t, 0)
-            stage1(b, t, 1)
-            if b == 0:
-                cast_w1(1, t, 0)
-                cast_w1(1, t, 1)
-                quantise_w1(1, t)
-            else:
-                cast_wo(t // 2, t % 2)
-                if t % 2 == 1:
-                    quantise_wo(t // 2)
+            stage1(b, t, first_pass_first if n == 0 else by_half)
             if n == 0:
-                deal_w2_words(1)
-            if 1 <= n <= 6:
-                pb, pt = slices[n - 1]
-                difference(pb, pt, 0, PAIRS)
-            if n == 5:
-                quantise_d(0, 0, PAIRS)
-        half = PAIRS // 2
-        for m0 in (0, half):
-            difference(1, 2, m0, m0 + half)
-            difference(1, 3, m0, m0 + half)
-        for m0 in (0, half):
-            quantise_d(1, m0, m0 + half)
-            for j in range(4):
-                stage2(j, m0, m0 + half)
-        for j in range(4):
+                cast_w1(0, 1, 0, nc.vector.tensor_copy)
+                cast_w1(0, 1, 1, nc.vector.tensor_copy)
+                quantise_w1(0, 1)
+            if n + 2 < len(slices):
+                nb, nt = slices[n + 2]
+                cast_w1(nb, nt, 0)
+                cast_w1(nb, nt, 1)
+                quantise_w1(nb, nt)
+            if n == 1:
+                turn_vectors()
+            for k in range(WO_SHARE[n]):
+                wb, part = wo_parts.pop(0)
+                cast_wo(wb, part)
+                if part == 3:
+                    quantise_wo(wb)
+            if 2 <= n <= 5:
+                scale(*slices[n - 2], 0, PAIRS, diffs[n - 2])
+            if 1 <= n <= 5:
+                diffs[n - 1] = difference(*slices[n - 1], 0, PAIRS, PARTS, diffs.get(n - 2))
+        diffs[5] = difference(*slices[5], 0, PAIRS, PARTS)
+        weave(0, 0, 256)
+        scale(*slices[4], 0, PAIRS, diffs[4])
+        weave(0, 256, PAIRS)
+        scale(*slices[5], 0, PAIRS, diffs[5])
+        quantise_d(0, 0, PAIRS)
+        last0 = PIECES[-1][0]
+        acc = [bank() for j in range(4)]
+        early = bank()
+        for m0, m1 in PIECES[:-1]:
+            stage2(early, 0, 0, m0, m1, 0, m0 == 0, False)
+        stage2(acc[0], 0, 0, last0, PAIRS, last0, True, False)
+        for j in range(1, 4):
+            stage2(acc[j], j, 0, 0, PAIRS, 0, True, False)
+
+        def tail_piece(m0, m1):
+            quantise_d(1, m0, m1)
+            if m1 == PAIRS:
+                stage2(acc[0], 0, 1, m0, m1, m0, False, True)
+            else:
+                stage2(early, 0, 1, m0, m1, 0, False, m1 == last0)
+            for j in range(1, 4):
+                stage2(acc[j], j, 1, m0, m1, 0, False, m1 == PAIRS)
+
+        for k, (m0, m1) in enumerate(PIECES):
+            pair = [difference(1, t, m0, m1, 1) for t in (2, 3)]
+            if k > 0:
+                tail_piece(*PIECES[k - 1])
+            scale(1, 2, m0, m1, pair[0])
+            scale(1, 3, m0, m1, pair[1])
+            weave(1, m0, m1)
+        tail_piece(*PIECES[-1])
+        finish(early, 0, 0, last0)
+        finish(acc[0], 0, last0, PAIRS)
+        mates(0)
+        for j in range(1, 4):
+            finish(acc[j], j, 0, PAIRS)
             mates(j)

@@ -24,6 +24,8 @@ BANK = 512
 RUN = 8
 WO_SHARE = (0, 0, 0, 1, 1, 1, 0, 5)
 PARTS = 2
+DIFF_BUFS = 6
+TAB_SPLIT = 1280
 PIECES = ((0, 128), (128, 256), (256, 384), (384, 512))
 
 
@@ -43,17 +45,18 @@ def tile_list_cheese_wheel_faces_kernel(
         def load_list(name, src):
             nc.sync.dma_start(lists[name][:], src)
 
-        tab_s = work.tile([P, T], U8, name="tab_s", tag="early", bufs=1, align_bytes=64)
+        tab_s = keep.tile([P, T], U8, name="tab_s", align_bytes=64)
         tab_w = [keep.tile([P, T], I32, name="tab_w%d" % a, align_bytes=64) for a in range(2)]
         picked_s = keep.tile([P, S], U8, name="picked_s", align_bytes=64)
         stage = keep.tile([P, 512], I32, name="stage")
         planes = keep.tile([P, 2, 512], I32, name="planes", align_bytes=64)
         v_w = [[keep.tile([P, BANK], U32, name="v_w%d%d" % (a, c), align_bytes=64) for c in range(2)] for a in range(2)]
         w1_raw = {}
-        w2_raw = keep.tile([P, 2, 512], I32, name="w2_raw", align_bytes=64)
+        w2_raw = [keep.tile([P, 2, 256], I32, name="w2_raw%d" % b, align_bytes=64) for b in range(2)]
         w2_dealt = keep.tile([P, 2, 256], I32, name="w2_dealt", align_bytes=64)
         w2s_dealt = keep.tile([P, 2, 128], I32, name="w2s_dealt", align_bytes=64)
         wo_all = {}
+        vec_rows = keep.tile([P, P], F32, name="vec_rows")
         ident = keep.tile([P, P], F32, name="ident")
         vec = keep.tile([P, 12], F32, name="vec")
 
@@ -63,6 +66,8 @@ def tile_list_cheese_wheel_faces_kernel(
         nc.gpsimd.memset(tab_s[0:96, :].bitcast(I32), 0)
         nc.gpsimd.memset(planes[:], 0)
         make_identity(nc, ident[:])
+        nc.gpsimd.memset(vec_rows[0:96, :], 0.0)
+        nc.gpsimd.memset(vec_rows[96:116, :], 0.0)
 
         def load_w1(first, count):
             for a in range(2):
@@ -72,8 +77,11 @@ def tile_list_cheese_wheel_faces_kernel(
                     w1[PASS * a : PASS * (a + 1), P * first : P * (first + count)].rearrange("(p j) c -> p j c", j=PACK),
                 )
 
-        def load_tab(a):
-            nc.sync.dma_start(tab_w[a][:], tab_words[a].rearrange("p t i -> p (t i)").bitcast(I32))
+        def load_tab(a, c0, c1):
+            nc.sync.dma_start(tab_w[a][:, c0:c1], tab_words[a].rearrange("p t i -> p (t i)").bitcast(I32)[:, c0:c1])
+
+        def load_w2(b):
+            nc.sync.dma_start(w2_raw[b][:], w2_words.bitcast(I32).rearrange("a p c -> p a c")[:, :, 256 * b : 256 * (b + 1)])
 
         def load_wo():
             for b in range(2):
@@ -86,30 +94,29 @@ def tile_list_cheese_wheel_faces_kernel(
         load_list("offs", offs)
         nc.sync.dma_start(tab_s[96:128, :].bitcast(I32), tab_scales.bitcast(I32).rearrange("a q c -> q a c"))
         nc.sync.dma_start(stage[96:128, 256:512], w2_scales.bitcast(I32).rearrange("a q c -> q a c"))
+        load_tab(0, 0, TAB_SPLIT)
+        load_tab(0, TAB_SPLIT, T)
+        load_w1(0, 1)
+        load_tab(1, 0, T)
+        load_w2(0)
         load_list("pos1", pos1)
         load_list("pos2", pos2)
-        load_list("pos3", pos3)
-        load_list("pos4", pos4)
-        load_tab(0)
-        load_w1(0, 1)
-        load_tab(1)
-        nc.sync.dma_start(w2_raw[:], w2_words.bitcast(I32).rearrange("a p c -> p a c"))
-        load_w1(1, 1)
 
         nc.vector.tensor_copy(picked_s[:], tab_s[:].indirect(lists["offs"][:]))
         nc.vector.tensor_copy(stage[96:128, 0:256], picked_s[96:128, :].bitcast(I32))
         for q in range(4):
-            (nc.gpsimd, nc.scalar)[q % 2].dma_start(planes[32 * q : 32 * q + 4, :, :], stage[96 + 8 * q : 96 + 8 * q + 8, :])
+            nc.sync.dma_start(planes[32 * q : 32 * q + 4, :, :], stage[96 + 8 * q : 96 + 8 * q + 8, :])
 
+        load_w1(1, 1)
         load_w1(2, 2)
+        load_w2(1)
+        nc.sync.dma_start(vec_rows[116:120, :], gain[0:PASS].rearrange("(t p) -> t p", p=P))
+        nc.sync.dma_start(vec_rows[120:124, :], gain[PASS : 2 * PASS].rearrange("(g t i) -> t g i", t=PACK, i=RUN))
+        nc.sync.dma_start(vec_rows[124:128, :], bo.rearrange("(j p) -> j p", p=P))
         load_w1(4, 4)
         load_wo()
-
-        vec_rows = work.tile([P, P], F32, name="vec_rows", tag="early", bufs=1, align_bytes=64)
-        nc.gpsimd.memset(vec_rows[:], 0.0)
-        nc.gpsimd.dma_start(vec_rows[0:4, :], gain[0:PASS].rearrange("(t p) -> t p", p=P))
-        nc.gpsimd.dma_start(vec_rows[4:8, :], gain[PASS : 2 * PASS].rearrange("(g t i) -> t g i", t=PACK, i=RUN))
-        nc.gpsimd.dma_start(vec_rows[8:12, :], bo.rearrange("(j p) -> j p", p=P))
+        load_list("pos3", pos3)
+        load_list("pos4", pos4)
 
         def gather_words(a, c):
             nc.vector.tensor_copy(
@@ -119,33 +126,29 @@ def tile_list_cheese_wheel_faces_kernel(
         def deal_w2():
             nc.vector.tensor_copy(
                 w2_dealt[:].rearrange("p a (t g w) -> p a t g w", t=PACK, w=4),
-                w2_raw[:, :, 256:512].rearrange("p a (g t w) -> p a t g w", t=PACK, w=4),
+                w2_raw[1][:].rearrange("p a (g t w) -> p a t g w", t=PACK, w=4),
             )
             nc.vector.tensor_copy(
                 w2s_dealt[:].rearrange("p a (t g w) -> p a t g w", t=PACK, w=2),
                 planes[:, :, 384:512].rearrange("p a (g t w) -> p a t g w", t=PACK, w=2),
             )
 
-        w2_w = [w2_raw[:, :, 0:256], w2_dealt[:]]
+        w2_w = [w2_raw[0][:], w2_dealt[:]]
         w2_s = [planes[:, :, 256:384], w2s_dealt[:]]
 
         w1_w = {}
         w1_s = {}
         w1_bf = {}
 
-        def cast_w1(b, t, a, copy=nc.scalar.copy):
-            if a == 0:
+        def cast_w1(b, t, a, copy=nc.scalar.copy, part=slice(0, 16)):
+            if (b, t) not in w1_bf:
                 w1_bf[b, t] = work.tile([P, 2, PASS], BF16, name="w1_bf", tag="ring", bufs=3, align_bytes=64)
             if b == 0:
-                copy(
-                    w1_bf[b, t][:, a, :].rearrange("p (c i j) -> p c j i", i=4, j=PACK),
-                    w1_raw[min(t, 2), a][:, :, P * max(t - 2, 0) : P * max(t - 1, 1)].rearrange("p j (c i) -> p c j i", i=4),
-                )
+                source = w1_raw[min(t, 2), a][:, :, P * max(t - 2, 0) : P * max(t - 1, 1)]
+                source = source.rearrange("p j (g u i) -> p g u j i", u=2, i=4)
             else:
-                nc.scalar.copy(
-                    w1_bf[b, t][:, a, :].rearrange("p (g u i j) -> p g u j i", u=2, i=4, j=PACK),
-                    w1_raw[4, a][:].rearrange("p j (g t u i) -> p t g u j i", t=PACK, u=2, i=4)[:, t],
-                )
+                source = w1_raw[4, a][:].rearrange("p j (g t u i) -> p t g u j i", t=PACK, u=2, i=4)[:, t]
+            copy(w1_bf[b, t][:, a, :].rearrange("p (g u i j) -> p g u j i", u=2, i=4, j=PACK)[:, part], source[:, part])
 
         def quantise_w1(b, t):
             w1_w[b, t] = work.tile([P, 2 * P], U32, name="w1_w", tag="ring", bufs=3, align_bytes=64)
@@ -156,8 +159,8 @@ def tile_list_cheese_wheel_faces_kernel(
                 in_=w1_bf[b, t][:].rearrange("p a c -> p (a c)"),
             )
 
-        wo_w = [keep.tile([P, N], U32, name="wo_w%d" % b, align_bytes=64) for b in range(2)]
-        wo_s = [keep.tile([P, N], U8, name="wo_s%d" % b, align_bytes=64) for b in range(2)]
+        wo_w = {}
+        wo_s = {}
         wo_bf = [keep.tile([P, PACK * N], BF16, name="wo_bf%d" % b, align_bytes=64) for b in range(2)]
 
         def cast_wo(b, part):
@@ -167,8 +170,18 @@ def tile_list_cheese_wheel_faces_kernel(
                 wo_all[b][:].rearrange("p t (c i) -> p c t i", i=4)[:, cols],
             )
 
-        def quantise_wo(b):
-            nc.vector.quantize_mx(out=wo_w[b][:].bitcast(FP8X4), scales=wo_s[b][:], in_=wo_bf[b][:])
+        def quantise_wo(b, first, count):
+            if first == 0:
+                words = keep.tile([P, P], U32, name="wo_w%d" % b, align_bytes=64)
+            else:
+                words = work.tile([P, count * P], U32, name="wo_late", tag="diff", bufs=DIFF_BUFS, align_bytes=64)
+            scales = keep.tile([P, count * P], U8, name="wo_s%d%d" % (b, first), align_bytes=64)
+            nc.vector.quantize_mx(
+                out=words[:].bitcast(FP8X4), scales=scales[:], in_=wo_bf[b][:, PASS * first : PASS * (first + count)]
+            )
+            for j in range(count):
+                wo_w[b, first + j] = words[:, P * j : P * (j + 1)]
+                wo_s[b, first + j] = scales[:, P * j : P * (j + 1)]
 
         h = {}
         bank_count = [0]
@@ -211,7 +224,7 @@ def tile_list_cheese_wheel_faces_kernel(
             step = width // parts
             if second is None:
                 second = work.tile([P, width], F32, name="second", bufs=4)
-            diff = work.tile([P, width], F32, name="diff", bufs=6)
+            diff = work.tile([P, width], F32, name="diff", tag="diff", bufs=DIFF_BUFS, align_bytes=64)
             for u in range(parts):
                 cols = slice((m0 + u * step) // 16, (m0 + (u + 1) * step) // 16)
                 nc.vector.tensor_copy(second[:, u * step : (u + 1) * step], h[b, t][:].indirect(lists["pos2"][:, cols]))
@@ -252,8 +265,8 @@ def tile_list_cheese_wheel_faces_kernel(
         def stage2(acc, j, b, m0, m1, first, start, stop):
             nc.tensor.matmul_mx(
                 out=acc[:, m0 - first : m1 - first],
-                lhsT=wo_w[b][:, P * j : P * (j + 1)].bitcast(FP8X4),
-                lhsT_scale=wo_s[b][:, P * j : P * (j + 1)],
+                lhsT=wo_w[b, j].bitcast(FP8X4),
+                lhsT_scale=wo_s[b, j],
                 rhs=d_w[b][:, m0:m1].bitcast(FP8X4),
                 rhs_scale=d_s[b][:, m0:m1],
                 start=start,
@@ -275,7 +288,7 @@ def tile_list_cheese_wheel_faces_kernel(
         def turn_vectors():
             turned = bank()
             nc.tensor.transpose(turned[:, 0:P], vec_rows[:], ident[:])
-            nc.scalar.copy(vec[:], turned[:, 0:12])
+            nc.scalar.copy(vec[:], turned[:, 116:128])
 
         gather_words(0, 0)
         gather_words(0, 1)
@@ -284,11 +297,10 @@ def tile_list_cheese_wheel_faces_kernel(
         quantise_w1(0, 0)
         gather_words(1, 0)
         gather_words(1, 1)
-        deal_w2()
 
         slices = [(b, t) for b in range(2) for t in range(PACK)]
         by_half = [(kind, c, a) for c in range(2) for kind in range(2) for a in range(2)]
-        first_pass_first = [x for x in by_half if x[2] == 0] + [x for x in by_half if x[2] == 1]
+        first_pass_first = [(kind, c, a) for c in range(2) for a in range(2) for kind in range(2)]
         wo_parts = [(b, part) for b in range(2) for part in range(4)]
         diffs = {}
         for n, (b, t) in enumerate(slices):
@@ -304,11 +316,12 @@ def tile_list_cheese_wheel_faces_kernel(
                 quantise_w1(nb, nt)
             if n == 1:
                 turn_vectors()
+                deal_w2()
             for k in range(WO_SHARE[n]):
                 wb, part = wo_parts.pop(0)
                 cast_wo(wb, part)
-                if part == 3:
-                    quantise_wo(wb)
+                if part == 0:
+                    quantise_wo(wb, 0, 1)
             if 2 <= n <= 5:
                 scale(*slices[n - 2], 0, PAIRS, diffs[n - 2])
             if 1 <= n <= 5:
@@ -325,8 +338,6 @@ def tile_list_cheese_wheel_faces_kernel(
         for m0, m1 in PIECES[:-1]:
             stage2(early, 0, 0, m0, m1, 0, m0 == 0, False)
         stage2(acc[0], 0, 0, last0, PAIRS, last0, True, False)
-        for j in range(1, 4):
-            stage2(acc[j], j, 0, 0, PAIRS, 0, True, False)
 
         def tail_piece(m0, m1):
             quantise_d(1, m0, m1)
@@ -334,8 +345,6 @@ def tile_list_cheese_wheel_faces_kernel(
                 stage2(acc[0], 0, 1, m0, m1, m0, False, True)
             else:
                 stage2(early, 0, 1, m0, m1, 0, False, m1 == last0)
-            for j in range(1, 4):
-                stage2(acc[j], j, 1, m0, m1, 0, False, m1 == PAIRS)
 
         for k, (m0, m1) in enumerate(PIECES):
             pair = [difference(1, t, m0, m1, 1) for t in (2, 3)]
@@ -344,7 +353,12 @@ def tile_list_cheese_wheel_faces_kernel(
             scale(1, 2, m0, m1, pair[0])
             scale(1, 3, m0, m1, pair[1])
             weave(1, m0, m1)
+        quantise_wo(0, 1, 3)
+        quantise_wo(1, 1, 3)
         tail_piece(*PIECES[-1])
+        for j in range(1, 4):
+            for b in range(2):
+                stage2(acc[j], j, b, 0, PAIRS, 0, b == 0, b == 1)
         finish(early, 0, 0, last0)
         finish(acc[0], 0, last0, PAIRS)
         mates(0)

from contextlib import ExitStack

import concourse.mybir as mybir
from concourse.masks import make_identity

K, H, N, T, S, PAIRS, MATES = 1024, 1024, 512, 2048, 1024, 512, 256
FLOPS = 2 * (2 * K * H * S + H * N * PAIRS)

F32 = mybir.dt.float32
BF16 = mybir.dt.bfloat16
I32 = mybir.dt.int32
U32 = mybir.dt.uint32
U16 = mybir.dt.uint16
U8 = mybir.dt.uint8
FP8X4 = mybir.dt.float8_e4m3fn_x4
FP4X4 = mybir.dt.float4_e2m1fn_x4
ACT = mybir.ActivationFunctionType
ALU = mybir.AluOpType

P = 128
PACK = 4
PASS = P * PACK
BANK = 512
RUN = 8
WO_SHARE = (0, 0, 0, 1, 1, 1, 0, 5)
PARTS = 2
DIFF_BUFS = 6
TAB_SPLIT = 1280
PIECES = ((0, 128), (128, 256), (256, 384), (384, 512))


def tile_list_cheese_wheel_faces_kernel(
    tc, tab_words, tab_scales, offs, pos1, pos2, pos3, pos4, w1, w2_words, w2_scales, gain, wo, bo, out
):
    nc = tc.nc
    with ExitStack() as ctx:
        keep = ctx.enter_context(tc.tile_pool(name="keep", bufs=1))
        work = ctx.enter_context(tc.tile_pool(name="work", bufs=2))
        psum = ctx.enter_context(tc.psum_pool(name="psum", bufs=1))

        lists = {}
        for name, src in (("offs", offs), ("pos1", pos1), ("pos2", pos2), ("pos3", pos3), ("pos4", pos4)):
            lists[name] = keep.tile(list(src.shape), U16, name="list_" + name)

        def load_list(name, src):
            nc.sync.dma_start(lists[name][:], src)

        tab_s = keep.tile([P, T], U8, name="tab_s", align_bytes=64)
        tab_w = [keep.tile([P, T], I32, name="tab_w%d" % a, align_bytes=64) for a in range(2)]
        picked_s = keep.tile([P, S], U8, name="picked_s", align_bytes=64)
        stage = keep.tile([P, 512], I32, name="stage")
        planes = keep.tile([P, 2, 512], I32, name="planes", align_bytes=64)
        v_w = [[keep.tile([P, BANK], U32, name="v_w%d%d" % (a, c), align_bytes=64) for c in range(2)] for a in range(2)]
        w1_raw = {}
        w2_raw = [keep.tile([P, 2, 256], I32, name="w2_raw%d" % b, align_bytes=64) for b in range(2)]
        w2_dealt = keep.tile([P, 2, 256], I32, name="w2_dealt", align_bytes=64)
        w2s_dealt = keep.tile([P, 2, 128], I32, name="w2s_dealt", align_bytes=64)
        wo_all = {}
        vec_rows = keep.tile([P, P], F32, name="vec_rows")
        ident = keep.tile([P, P], F32, name="ident")
        vec = keep.tile([P, 12], F32, name="vec")

        warm = keep.tile([P, 16], F32, name="warm")
        nc.gpsimd.memset(warm[:, 0:8], 0.0)
        nc.scalar.activation(warm[:, 8:9], warm[:, 0:1], ACT.Tanh)
        nc.gpsimd.memset(tab_s[0:96, :].bitcast(I32), 0)
        nc.gpsimd.memset(planes[:], 0)
        make_identity(nc, ident[:])
        nc.gpsimd.memset(vec_rows[0:96, :], 0.0)
        nc.gpsimd.memset(vec_rows[96:116, :], 0.0)

        def load_w1(first, count):
            for a in range(2):
                w1_raw[first, a] = keep.tile([P, PACK, count * P], F32, name="w1_raw%d%d" % (first, a))
                nc.sync.dma_start(
                    w1_raw[first, a][:],
                    w1[PASS * a : PASS * (a + 1), P * first : P * (first + count)].rearrange("(p j) c -> p j c", j=PACK),
                )

        def load_tab(a, c0, c1):
            nc.sync.dma_start(tab_w[a][:, c0:c1], tab_words[a].rearrange("p t i -> p (t i)").bitcast(I32)[:, c0:c1])

        def load_w2(b):
            nc.sync.dma_start(w2_raw[b][:], w2_words.bitcast(I32).rearrange("a p c -> p a c")[:, :, 256 * b : 256 * (b + 1)])

        def load_wo():
            for b in range(2):
                wo_all[b] = keep.tile([P, PACK, N], F32, name="wo_raw%d" % b)
            nc.sync.dma_start(wo_all[0][:], wo[0:PASS, :].rearrange("(p t) n -> p t n", t=PACK))
            rows = wo[PASS : 2 * PASS, :].rearrange("(g t i) n -> t g i n", t=PACK, i=RUN)
            for t in range(PACK):
                nc.sync.dma_start(wo_all[1][:, t, :], rows[t])

        load_list("offs", offs)
        nc.sync.dma_start(tab_s[96:128, :].bitcast(I32), tab_scales.bitcast(I32).rearrange("a q c -> q a c"))
        nc.sync.dma_start(stage[96:128, 256:512], w2_scales.bitcast(I32).rearrange("a q c -> q a c"))
        load_tab(0, 0, TAB_SPLIT)
        load_tab(0, TAB_SPLIT, T)
        load_w1(0, 1)
        load_tab(1, 0, T)
        load_w2(0)
        load_list("pos1", pos1)
        load_list("pos2", pos2)

        nc.vector.tensor_copy(picked_s[:], tab_s[:].indirect(lists["offs"][:]))
        nc.vector.tensor_copy(stage[96:128, 0:256], picked_s[96:128, :].bitcast(I32))
        for q in range(4):
            nc.sync.dma_start(planes[32 * q : 32 * q + 4, :, :], stage[96 + 8 * q : 96 + 8 * q + 8, :])

        load_w1(1, 1)
        load_w1(2, 2)
        load_w2(1)
        nc.sync.dma_start(vec_rows[116:120, :], gain[0:PASS].rearrange("(t p) -> t p", p=P))
        nc.sync.dma_start(vec_rows[120:124, :], gain[PASS : 2 * PASS].rearrange("(g t i) -> t g i", t=PACK, i=RUN))
        nc.sync.dma_start(vec_rows[124:128, :], bo.rearrange("(j p) -> j p", p=P))
        load_w1(4, 4)
        load_wo()
        load_list("pos3", pos3)
        load_list("pos4", pos4)

        def gather_words(a, c):
            nc.vector.tensor_copy(
                v_w[a][c][:], tab_w[a][:].bitcast(U32).indirect(lists["offs"][:, 32 * c : 32 * (c + 1)])
            )

        def deal_w2():
            nc.vector.tensor_copy(
                w2_dealt[:].rearrange("p a (t g w) -> p a t g w", t=PACK, w=4),
                w2_raw[1][:].rearrange("p a (g t w) -> p a t g w", t=PACK, w=4),
            )
            nc.vector.tensor_copy(
                w2s_dealt[:].rearrange("p a (t g w) -> p a t g w", t=PACK, w=2),
                planes[:, :, 384:512].rearrange("p a (g t w) -> p a t g w", t=PACK, w=2),
            )

        w2_w = [w2_raw[0][:], w2_dealt[:]]
        w2_s = [planes[:, :, 256:384], w2s_dealt[:]]

        w1_w = {}
        w1_s = {}
        w1_bf = {}

        def cast_w1(b, t, a, copy=nc.scalar.copy, part=slice(0, 16)):
            if (b, t) not in w1_bf:
                w1_bf[b, t] = work.tile([P, 2, PASS], BF16, name="w1_bf", tag="ring", bufs=3, align_bytes=64)
            if b == 0:
                source = w1_raw[min(t, 2), a][:, :, P * max(t - 2, 0) : P * max(t - 1, 1)]
                source = source.rearrange("p j (g u i) -> p g u j i", u=2, i=4)
            else:
                source = w1_raw[4, a][:].rearrange("p j (g t u i) -> p t g u j i", t=PACK, u=2, i=4)[:, t]
            copy(w1_bf[b, t][:, a, :].rearrange("p (g u i j) -> p g u j i", u=2, i=4, j=PACK)[:, part], source[:, part])

        def quantise_w1(b, t):
            w1_w[b, t] = work.tile([P, 2 * P], U32, name="w1_w", tag="ring", bufs=3, align_bytes=64)
            w1_s[b, t] = keep.tile([P, 2 * P], U8, name="w1_s%d%d" % (b, t), align_bytes=64)
            nc.vector.quantize_mx(
                out=w1_w[b, t][:].bitcast(FP8X4),
                scales=w1_s[b, t][:],
                in_=w1_bf[b, t][:].rearrange("p a c -> p (a c)"),
            )

        wo_w = {}
        wo_s = {}
        wo_bf = [keep.tile([P, PACK * N], BF16, name="wo_bf%d" % b, align_bytes=64) for b in range(2)]

        def cast_wo(b, part):
            cols = slice(part * 32, (part + 1) * 32)
            nc.scalar.copy(
                wo_bf[b][:].rearrange("p (c i t) -> p c t i", i=4, t=PACK)[:, cols],
                wo_all[b][:].rearrange("p t (c i) -> p c t i", i=4)[:, cols],
            )

        def quantise_wo(b, first, count):
            if first == 0:
                words = keep.tile([P, P], U32, name="wo_w%d" % b, align_bytes=64)
            else:
                words = work.tile([P, count * P], U32, name="wo_late", tag="diff", bufs=DIFF_BUFS, align_bytes=64)
            scales = keep.tile([P, count * P], U8, name="wo_s%d%d" % (b, first), align_bytes=64)
            nc.vector.quantize_mx(
                out=words[:].bitcast(FP8X4), scales=scales[:], in_=wo_bf[b][:, PASS * first : PASS * (first + count)]
            )
            for j in range(count):
                wo_w[b, first + j] = words[:, P * j : P * (j + 1)]
                wo_s[b, first + j] = scales[:, P * j : P * (j + 1)]

        h = {}
        bank_count = [0]

        def bank():
            bank_count[0] = bank_count[0] + 1
            return psum.tile([P, BANK], F32, name="bank", tag="bank%d" % (bank_count[0] % 8))

        def stage1(b, t, order):
            h[b, t] = work.tile([P, S], F32, name="h", bufs=4)
            banks = {(kind, c): bank() for c in range(2) for kind in range(2)}
            for kind, c, a in order:
                if kind == 0:
                    words = w1_w[b, t][:, P * a : P * (a + 1)].bitcast(FP8X4)
                    scales = w1_s[b, t][:, P * a : P * (a + 1)]
                else:
                    words = w2_w[b][:, a, 64 * t : 64 * (t + 1)].bitcast(U8).bitcast(FP4X4)
                    scales = w2_s[b][:, a, 32 * t : 32 * (t + 1)].bitcast(U8)
                nc.tensor.matmul_mx(
                    out=banks[kind, c][:],
                    lhsT=words,
                    lhsT_scale=scales,
                    rhs=v_w[a][c][:].bitcast(FP8X4),
                    rhs_scale=planes[:, a, P * c : P * (c + 1)].bitcast(U8),
                    start=(a == 0),
                    stop=(a == 1),
                )
            for c in range(2):
                th = work.tile([P, BANK], F32, name="th", bufs=4)
                nc.scalar.activation(th[:], banks[0, c][:], ACT.Tanh)
                nc.vector.tensor_tensor(h[b, t][:, BANK * c : BANK * (c + 1)], banks[1, c][:], th[:], ALU.add)

        d_rows = [keep.tile([P, PACK, PAIRS], BF16, name="d_rows%d" % b) for b in range(2)]
        woven = [keep.tile([P, PAIRS, PACK], BF16, name="woven%d" % b, align_bytes=64) for b in range(2)]
        d_w = [keep.tile([P, PAIRS], U32, name="d_w%d" % b, align_bytes=64) for b in range(2)]
        d_s = [keep.tile([P, PAIRS], U8, name="d_s%d" % b, align_bytes=64) for b in range(2)]

        def difference(b, t, m0, m1, parts, second=None):
            width = m1 - m0
            step = width // parts
            if second is None:
                second = work.tile([P, width], F32, name="second", bufs=4)
            diff = work.tile([P, width], F32, name="diff", tag="diff", bufs=DIFF_BUFS, align_bytes=64)
            for u in range(parts):
                cols = slice((m0 + u * step) // 16, (m0 + (u + 1) * step) // 16)
                nc.vector.tensor_copy(second[:, u * step : (u + 1) * step], h[b, t][:].indirect(lists["pos2"][:, cols]))
            for u in range(parts):
                cols = slice((m0 + u * step) // 16, (m0 + (u + 1) * step) // 16)
                nc.vector.tensor_tensor(
                    diff[:, u * step : (u + 1) * step],
                    h[b, t][:].indirect(lists["pos1"][:, cols]),
                    second[:, u * step : (u + 1) * step],
                    ALU.subtract,
                )
            return diff

        def scale(b, t, m0, m1, diff):
            factor = vec[:, 4 * b + t : 4 * b + t + 1]
            if b == 0:
                rows = work.tile([P, PAIRS], BF16, name="rows", bufs=4)
                nc.scalar.activation(rows[:], diff[:], ACT.Copy, scale=factor)
                nc.sync.dma_start(d_rows[0][32 * t : 32 * (t + 1), :, :], rows[:])
            else:
                nc.scalar.activation(d_rows[1][:, t, m0:m1], diff[:], ACT.Copy, scale=factor)

        def weave(b, m0, m1):
            nc.scalar.copy(
                woven[b][:, m0:m1, :].rearrange("p (c i) t -> p c t i", i=4),
                d_rows[b][:, :, m0:m1].rearrange("p t (c i) -> p c t i", i=4),
            )

        def quantise_d(b, m0, m1):
            nc.vector.quantize_mx(
                out=d_w[b][:, m0:m1].bitcast(FP8X4),
                scales=d_s[b][:, m0:m1],
                in_=woven[b][:, m0:m1, :].rearrange("p m t -> p (m t)"),
            )

        y = [keep.tile([P, PAIRS], F32, name="y%d" % j) for j in range(4)]

        def stage2(acc, j, b, m0, m1, first, start, stop):
            nc.tensor.matmul_mx(
                out=acc[:, m0 - first : m1 - first],
                lhsT=wo_w[b, j].bitcast(FP8X4),
                lhsT_scale=wo_s[b, j],
                rhs=d_w[b][:, m0:m1].bitcast(FP8X4),
                rhs_scale=d_s[b][:, m0:m1],
                start=start,
                stop=stop,
            )

        def finish(acc, j, m0, m1):
            nc.scalar.activation(y[j][:, m0:m1], acc[:, 0 : m1 - m0], ACT.Tanh, bias=vec[:, 8 + j : 9 + j])

        def mates(j):
            left = work.tile([P, MATES], F32, name="left")
            right = work.tile([P, MATES], F32, name="right")
            least = work.tile([P, MATES], F32, name="least", bufs=4)
            nc.vector.tensor_copy(left[:], y[j][:].indirect(lists["pos3"][:]))
            nc.vector.tensor_copy(right[:], y[j][:].indirect(lists["pos4"][:]))
            nc.vector.tensor_tensor(least[:], left[:], right[:], ALU.min)
            nc.sync.dma_start(out[P * j : P * (j + 1), :], least[:])

        def turn_vectors():
            turned = bank()
            nc.tensor.transpose(turned[:, 0:P], vec_rows[:], ident[:])
            nc.scalar.copy(vec[:], turned[:, 116:128])

        gather_words(0, 0)
        gather_words(0, 1)
        cast_w1(0, 0, 0)
        cast_w1(0, 0, 1)
        quantise_w1(0, 0)
        gather_words(1, 0)
        gather_words(1, 1)

        slices = [(b, t) for b in range(2) for t in range(PACK)]
        by_half = [(kind, c, a) for c in range(2) for kind in range(2) for a in range(2)]
        first_pass_first = [(kind, c, a) for c in range(2) for a in range(2) for kind in range(2)]
        wo_parts = [(b, part) for b in range(2) for part in range(4)]
        diffs = {}
        for n, (b, t) in enumerate(slices):
            stage1(b, t, first_pass_first if n == 0 else by_half)
            if n == 0:
                cast_w1(0, 1, 0, nc.vector.tensor_copy)
                cast_w1(0, 1, 1, nc.vector.tensor_copy)
                quantise_w1(0, 1)
            if n + 2 < len(slices):
                nb, nt = slices[n + 2]
                cast_w1(nb, nt, 0)
                cast_w1(nb, nt, 1)
                quantise_w1(nb, nt)
            if n == 1:
                turn_vectors()
                deal_w2()
            for k in range(WO_SHARE[n]):
                wb, part = wo_parts.pop(0)
                cast_wo(wb, part)
                if part == 0:
                    quantise_wo(wb, 0, 1)
            if 2 <= n <= 5:
                scale(*slices[n - 2], 0, PAIRS, diffs[n - 2])
            if 1 <= n <= 5:
                diffs[n - 1] = difference(*slices[n - 1], 0, PAIRS, PARTS, diffs.get(n - 2))
        diffs[5] = difference(*slices[5], 0, PAIRS, PARTS)
        weave(0, 0, 256)
        scale(*slices[4], 0, PAIRS, diffs[4])
        weave(0, 256, PAIRS)
        scale(*slices[5], 0, PAIRS, diffs[5])
        quantise_d(0, 0, PAIRS)
        last0 = PIECES[-1][0]
        acc = [bank() for j in range(4)]
        early = bank()
        for m0, m1 in PIECES[:-1]:
            stage2(early, 0, 0, m0, m1, 0, m0 == 0, False)
        stage2(acc[0], 0, 0, last0, PAIRS, last0, True, False)

        def tail_piece(m0, m1):
            quantise_d(1, m0, m1)
            if m1 == PAIRS:
                stage2(acc[0], 0, 1, m0, m1, m0, False, True)
            else:
                stage2(early, 0, 1, m0, m1, 0, False, m1 == last0)

        for k, (m0, m1) in enumerate(PIECES):
            pair = [difference(1, t, m0, m1, 1) for t in (2, 3)]
            if k > 0:
                tail_piece(*PIECES[k - 1])
            scale(1, 2, m0, m1, pair[0])
            scale(1, 3, m0, m1, pair[1])
            weave(1, m0, m1)
        quantise_wo(0, 1, 3)
        quantise_wo(1, 1, 3)
        tail_piece(*PIECES[-1])
        for j in range(1, 4):
            for b in range(2):
                stage2(acc[j], j, b, 0, PAIRS, 0, b == 0, b == 1)
        finish(early, 0, 0, last0)
        finish(acc[0], 0, last0, PAIRS)
        mates(0)
        for j in range(1, 4):
            finish(acc[j], j, 0, PAIRS)
            mates(j)
